import numpy as np
import ml_dtypes


def mxq(x, axis, fmt="e4m3"):
    dtype, down = {"e4m3": (ml_dtypes.float8_e4m3fn, 7), "e5m2": (ml_dtypes.float8_e5m2, 14)}[fmt]
    v = np.moveaxis(np.asarray(x, np.float32).astype(ml_dtypes.bfloat16).astype(np.float64), axis, -1)
    blocks = v.reshape(v.shape[:-1] + (-1, 32))
    amax = np.abs(blocks).max(-1, keepdims=True)
    byte = np.maximum(np.where(amax > 0, np.frexp(amax)[1] - 1 + 127, 0) - down, 1)
    scale = np.exp2(byte - 127.0)
    codes = (blocks / scale).astype(np.float32).astype(dtype).astype(np.float64)
    return np.moveaxis((codes * scale).reshape(v.shape), -1, axis)


WIDE = False


def mx_kscale(k):
    if not WIDE:
        return np.ones(k)
    levels = np.array([10, -10, 5, -5, 0])
    if k % 512:
        return np.exp2(np.random.permutation(np.resize(levels, k // 32))).repeat(32)
    a = np.empty((k // 512, 16))
    for p in range(k // 512):
        a[p, :8] = np.random.permutation(np.resize(levels, 8))
        for g in range(8):
            far = levels[np.abs(levels - a[p, g]) >= 10]
            a[p, g + 8] = far[np.random.randint(len(far))]
    return np.exp2(a.ravel()).repeat(32)


def f64(x):
    return np.asarray(x).astype(np.float64)


def striped(idx):
    return np.tile(idx.reshape(-1, 16).T, (8, 1)).astype(np.uint16)


def unstriped(offs):
    return offs[:16].T.reshape(-1).astype(np.int64)


def pack_weight(w):
    k, n = w.shape
    w = f64(np.asarray(w, np.float32).astype(ml_dtypes.bfloat16)).reshape(k // 32, 32, n)
    amax = np.abs(w).max(1)
    byte = np.clip(np.where(amax > 0, np.frexp(amax)[1] - 1 + 127 - 7, 1), 1, 254)
    scaled = (w * np.exp2(127.0 - byte)[:, None, :]).reshape(k, n).astype(np.float32)
    words = np.ascontiguousarray(scaled.reshape(k // 512, 128, 4, n).transpose(0, 1, 3, 2)).astype(ml_dtypes.float8_e4m3fn).view(np.uint8)
    return words, np.ascontiguousarray(byte.astype(np.uint8).reshape(k // 512, 16, n))


def unpack_weight(words, scales):
    g, p, n, _ = words.shape
    vals = np.ascontiguousarray(words).view(ml_dtypes.float8_e4m3fn).astype(np.float64) * np.repeat(np.exp2(scales.astype(np.float64) - 127.0), 8, axis=1)[..., None]
    return vals.transpose(0, 1, 3, 2).reshape(g * 512, n)

def planes(y):
    n, m = y.shape
    v = y.astype(np.float32).astype(ml_dtypes.bfloat16).astype(np.float64).reshape(n // 32, 32, m)
    top = np.abs(v).max(1)
    byte = np.clip(np.where(top > 0, np.frexp(top)[1] - 1 + 127 - 7, 1), 1, 254)
    codes = (v * np.exp2(127.0 - byte)[:, None, :]).reshape(n, m).astype(np.float32).astype(ml_dtypes.float8_e4m3fn).view(np.uint8)
    words = codes.reshape(n // 512, 128, 4, m).transpose(0, 1, 3, 2)
    return np.ascontiguousarray(words), np.ascontiguousarray(byte.astype(np.uint8).reshape(n // 512, 16, m))


K, T, S, H, U = 512, 2048, 512, 512, 1024


def setup_inputs():
    n = np.random.standard_normal
    s = mx_kscale(K)[:, None]
    u = mx_kscale(H)
    packed_xT = pack_weight(n((K, T)) * s)
    return {
        "x_words": packed_xT[0],
        "x_scales": packed_xT[1],
        "w1": (n((K, H)) / np.sqrt(K) / s * u).astype(np.float32),
        "w2": (n((H, H)) / np.sqrt(H) / u[:, None]).astype(np.float32),
        "skip": (n((H, U)) * u[:, None]).astype(np.float32),
        "offs": striped(np.random.permutation(T)[:S]),
        "cell": striped(np.random.permutation(U)[:S]),
    }


def reference(x_words, x_scales, w1, w2, skip, offs, cell):
    xq = unpack_weight(x_words, x_scales)[:, unstriped(offs)]
    up = np.zeros((H, U))
    up[:, unstriped(cell)] = mxq(f64(w1), 0, "e4m3").T @ xq
    z = up + f64(skip)
    out_0 = mxq(f64(w2), 0, "e4m3").T @ mxq(z, 0, "e4m3")
    return (out_0,) + planes(out_0)

@@ -1,0 +1,233 @@
+from contextlib import ExitStack
+
+import concourse.mybir as mybir
+
+K, T, S, H, U = 512, 2048, 512, 512, 1024
+FLOPS = 2 * K * H * S + 2 * H * H * U
+
+F32 = mybir.dt.float32
+BF16 = mybir.dt.bfloat16
+I32 = mybir.dt.int32
+U32 = mybir.dt.uint32
+U16 = mybir.dt.uint16
+U8 = mybir.dt.uint8
+FP8X4 = mybir.dt.float8_e4m3fn_x4
+ADD = mybir.AluOpType.add
+COPY = mybir.ActivationFunctionType.Copy
+
+P = 128
+PACK = 4
+HALF = S // 2
+CHUNK = 256
+GROUP = 128
+W1_SPLIT = 88
+W2_SPLIT = 64
+
+
+def tile_picked_unet_none_po_kernel(
+    tc, x_words, x_scales, w1, w2, skip, offs, cell, out_0, out_1, out_2
+):
+    nc = tc.nc
+    with ExitStack() as ctx:
+        keep = ctx.enter_context(tc.tile_pool(name="keep", bufs=1))
+        psum = ctx.enter_context(tc.psum_pool(name="psum", bufs=1))
+
+        def sb(name, shape, dtype, tag=None):
+            return keep.tile(shape, dtype, name=name, tag=tag or name, align_bytes=64)
+
+        offs_t = keep.tile([P, S // 16], U16, name="offs_t")
+        cell_t = keep.tile([P, S // 16], U16, name="cell_t")
+        x_table = sb("x_table", [P, T], U32)
+        xs_table = sb("xs_table", [P, T], U8)
+        w1_raw = sb("w1_raw", [P, PACK, H], F32)
+        windows = [sb("window%d" % t, [P, U], F32) for t in range(PACK)]
+
+        nc.vector.memset(xs_table[:].bitcast(I32), 0)
+        nc.sync.dma_start(out=offs_t[:], in_=offs)
+        nc.sync.dma_start(out=w1_raw[:], in_=w1.rearrange("(p j) c -> p j c", j=PACK))
+        for q in range(4):
+            nc.scalar.dma_start(
+                out=xs_table[32 * q : 32 * q + 4, :].bitcast(I32),
+                in_=x_scales[0, 4 * q : 4 * q + 4, :].bitcast(I32),
+            )
+        nc.sync.dma_start(
+            out=x_table[:].bitcast(I32),
+            in_=x_words[0].rearrange("p n t -> p (n t)").bitcast(I32),
+        )
+        nc.sync.dma_start(out=cell_t[:], in_=cell)
+
+        for t in range(PACK):
+            nc.vector.memset(windows[t][:], 0.0)
+
+        def deal_views(raw, dealt):
+            src = raw[:].rearrange("p j (m t) -> p m t j", t=PACK)
+            dst = dealt[:].rearrange("p (t m j) -> p m t j", t=PACK, j=PACK)
+            return src, dst
+
+        def quantize(codes, scales, values):
+            nc.vector.quantize_mx(out=codes.bitcast(FP8X4), scales=scales, in_=values)
+
+        xs = sb("xs", [P, S], U8)
+        nc.vector.tensor_copy(out=xs[:], in_=xs_table[:].indirect(offs_t[:]))
+
+        w1_dealt = sb("w1_dealt", [P, PACK * H], BF16)
+        w1_codes = sb("w1_codes", [P, H], U32)
+        w1_scales = sb("w1_scales", [P, H], U8)
+        src, dst = deal_views(w1_raw, w1_dealt)
+        nc.vector.tensor_copy(out=dst[:, :W1_SPLIT], in_=src[:, :W1_SPLIT])
+        nc.scalar.activation(out=dst[:, W1_SPLIT:], in_=src[:, W1_SPLIT:], func=COPY)
+        quantize(w1_codes[:], w1_scales[:], w1_dealt[:])
+
+        skip_rows = skip.rearrange("(p t) c -> p t c", t=PACK)
+        skip_a = sb("skip_a", [P, 2, U], F32, tag="xs_table")
+        nc.sync.dma_start(out=skip_a[:], in_=skip_rows[:, 0:2, :])
+        w2_raw = sb("w2_raw", [P, PACK, H], F32, tag="w1_raw")
+        nc.sync.dma_start(out=w2_raw[:], in_=w2.rearrange("(p j) c -> p j c", j=PACK))
+        skip_b = sb("skip_b", [P, 2, U], F32, tag="w1_dealt")
+        nc.sync.dma_start(out=skip_b[:], in_=skip_rows[:, 2:4, :])
+        skip_t = [skip_a, skip_b]
+
+        xw = [sb("xw%d" % s, [P, HALF], U32) for s in range(2)]
+        cols = HALF // 16
+        for s in range(2):
+            nc.vector.tensor_copy(out=xw[s][:], in_=x_table[:].indirect(offs_t[:, s * cols : (s + 1) * cols]))
+
+        h_bank = {}
+        for pair in range(2):
+            for s in range(2):
+                bank = psum.tile([P, 2, HALF], F32, name="h_bank%d%d" % (pair, s), tag="bank%d" % (2 * pair + s))
+                h_bank[pair, s] = bank
+                for i in range(2):
+                    t = 2 * pair + i
+                    nc.tensor.matmul_mx(
+                        out=bank[:, i, :],
+                        lhsT=w1_codes[:, t * P : (t + 1) * P].bitcast(FP8X4),
+                        lhsT_scale=w1_scales[:, t * P : (t + 1) * P],
+                        rhs=xw[s][:].bitcast(FP8X4),
+                        rhs_scale=xs[:, s * HALF : (s + 1) * HALF],
+                        start=True,
+                        stop=True,
+                    )
+        h = [sb("h%d" % pair, [P, 2, S], F32) for pair in range(2)]
+
+        def h_out(engine, pair, s):
+            dst = h[pair][:, :, s * HALF : (s + 1) * HALF]
+            if engine == "v":
+                nc.vector.tensor_copy(out=dst, in_=h_bank[pair, s][:])
+            else:
+                nc.scalar.copy(out=dst, in_=h_bank[pair, s][:])
+
+        def scatter(engine, t, lo, hi):
+            dst = windows[t][:].indirect(cell_t[:, lo // 16 : hi // 16])
+            src = h[t // 2][:, t % 2, lo:hi]
+            if engine == "v":
+                nc.vector.tensor_copy(out=dst, in_=src)
+            else:
+                nc.scalar.activation(out=dst, in_=src, func=COPY)
+
+        z_planes = sb("z_planes", [P, PACK, U], BF16)
+
+        def add_skip(t, lo, hi):
+            nc.vector.tensor_tensor(out=z_planes[:, t, lo:hi], in0=windows[t][:, lo:hi], in1=skip_t[t // 2][:, t % 2, lo:hi], op=ADD)
+
+        w2_dealt = sb("w2_dealt", [P, PACK * H], BF16)
+        w2_codes = sb("w2_codes", [P, H], U32)
+        w2_scales = sb("w2_scales", [P, H], U8)
+        src2, dst2 = deal_views(w2_raw, w2_dealt)
+
+        h_out("s", 0, 0)
+        h_out("v", 0, 1)
+        scatter("s", 1, 0, HALF)
+        scatter("v", 0, 0, S)
+        h_out("s", 1, 0)
+        h_out("s", 1, 1)
+        scatter("s", 1, HALF, S)
+        scatter("v", 2, 0, HALF)
+        scatter("s", 3, 0, HALF)
+        scatter("s", 2, HALF, S)
+        scatter("s", 3, HALF, S)
+        add_skip(0, 0, U)
+        add_skip(1, 0, U)
+        nc.vector.tensor_copy(out=dst2[:, :W2_SPLIT], in_=src2[:, :W2_SPLIT])
+        add_skip(2, 0, U)
+        nc.scalar.copy(out=dst2[:, W2_SPLIT:], in_=src2[:, W2_SPLIT:])
+
+        n_chunks = U // CHUNK
+        z_words = [sb("z_words%d" % c, [P, CHUNK * PACK], BF16) for c in range(n_chunks)]
+        z_codes = [sb("z_codes%d" % c, [P, CHUNK], U32) for c in range(n_chunks)]
+        z_scales = [sb("z_scales%d" % c, [P, CHUNK], U8) for c in range(n_chunks)]
+        y = [sb("y%d" % c, [P, PACK, CHUNK], F32) for c in range(n_chunks)]
+        y_words = [sb("y_words%d" % c, [P, CHUNK * PACK], BF16) for c in range(n_chunks)]
+        y_codes = sb("y_codes", [P, U], U32)
+        y_scales = sb("y_scales", [P, U], U8)
+        y_bank = {}
+        out_rows = out_0.rearrange("(p t) c -> p t c", t=PACK)
+        out_words = out_1[0].rearrange("p n t -> p (n t)").bitcast(I32)
+
+        def weave_z(c):
+            src = z_planes[:, :, c * CHUNK : (c + 1) * CHUNK].rearrange("p t (c i) -> p c t i", i=4)
+            dst = z_words[c][:].rearrange("p (c i t) -> p c t i", i=4, t=PACK)
+            nc.vector.tensor_copy(out=dst, in_=src)
+
+        def product(c):
+            for g in range(CHUNK // GROUP):
+                n = 2 * c + g
+                bank = psum.tile([P, PACK, GROUP], F32, name="y_bank%d" % n, tag="bank%d" % ((n + 4) % 8))
+                y_bank[c, g] = bank
+                for t in range(PACK):
+                    nc.tensor.matmul_mx(
+                        out=bank[:, t, :],
+                        lhsT=w2_codes[:, t * P : (t + 1) * P].bitcast(FP8X4),
+                        lhsT_scale=w2_scales[:, t * P : (t + 1) * P],
+                        rhs=z_codes[c][:, g * GROUP : (g + 1) * GROUP].bitcast(FP8X4),
+                        rhs_scale=z_scales[c][:, g * GROUP : (g + 1) * GROUP],
+                        start=True,
+                        stop=True,
+                    )
+
+        def y_out(c):
+            for g in range(CHUNK // GROUP):
+                nc.scalar.copy(out=y[c][:, :, g * GROUP : (g + 1) * GROUP], in_=y_bank[c, g][:])
+            nc.sync.dma_start(out=out_rows[:, :, c * CHUNK : (c + 1) * CHUNK], in_=y[c][:])
+
+        def weave_y_sbuf(c):
+            src = y[c][:].rearrange("p t (c i) -> p c t i", i=4)
+            dst = y_words[c][:].rearrange("p (c i t) -> p c t i", i=4, t=PACK)
+            nc.vector.tensor_copy(out=dst, in_=src)
+
+        def weave_y_psum(c):
+            for g in range(CHUNK // GROUP):
+                dst = y_words[c][:, g * GROUP * PACK : (g + 1) * GROUP * PACK].rearrange("p (c t) -> p c t", t=PACK)
+                nc.scalar.copy(out=dst, in_=y_bank[c, g][:].rearrange("p t c -> p c t"))
+
+        def quantize_y(c):
+            cs = slice(c * CHUNK, (c + 1) * CHUNK)
+            quantize(y_codes[:, cs], y_scales[:, cs], y_words[c][:])
+
+        add_skip(3, 0, CHUNK)
+        add_skip(3, CHUNK, 2 * CHUNK)
+        weave_z(0)
+        quantize(w2_codes[:], w2_scales[:], w2_dealt[:])
+        for c in range(n_chunks):
+            if c + 2 < n_chunks:
+                add_skip(3, (c + 2) * CHUNK, (c + 3) * CHUNK)
+            quantize(z_codes[c][:], z_scales[c][:], z_words[c][:])
+            if c + 1 < n_chunks:
+                weave_z(c + 1)
+            product(c)
+            y_out(c)
+        weave_y_psum(n_chunks - 1)
+        weave_y_sbuf(0)
+        for c in range(n_chunks):
+            if c + 1 < n_chunks - 1:
+                weave_y_sbuf(c + 1)
+            quantize_y(c)
+            if c % 2 == 1:
+                cs = slice((c - 1) * CHUNK, (c + 1) * CHUNK)
+                nc.sync.dma_start(out=out_words[:, cs], in_=y_codes[:, cs].bitcast(I32))
+        for q in range(4):
+            queue = nc.sync if q < 2 else nc.scalar
+            queue.dma_start(
+                out=out_2[0, 4 * q : 4 * q + 4, :].bitcast(I32),
+                in_=y_scales[32 * q : 32 * q + 4, :].bitcast(I32),
+            )

@@ -20,8 +20,8 @@ PACK = 4
 HALF = S // 2
 CHUNK = 256
 GROUP = 128
-W1_SPLIT = 88
-W2_SPLIT = 64
+T2_SPLIT = 128
+W1_SCALAR = 24
 
 
 def tile_picked_unet_none_po_kernel(
@@ -39,14 +39,16 @@ def tile_picked_unet_none_po_kernel(
         cell_t = keep.tile([P, S // 16], U16, name="cell_t")
         x_table = sb("x_table", [P, T], U32)
         xs_table = sb("xs_table", [P, T], U8)
-        w1_raw = sb("w1_raw", [P, PACK, H], F32)
+        w1_raw = [sb("w1_raw%d" % a, [P, PACK, H // 2], F32) for a in range(2)]
         windows = [sb("window%d" % t, [P, U], F32) for t in range(PACK)]
 
         nc.vector.memset(xs_table[:].bitcast(I32), 0)
         nc.sync.dma_start(out=offs_t[:], in_=offs)
-        nc.sync.dma_start(out=w1_raw[:], in_=w1.rearrange("(p j) c -> p j c", j=PACK))
+        w1_rows = w1.rearrange("(p j) c -> p j c", j=PACK)
+        for a in range(2):
+            nc.sync.dma_start(out=w1_raw[a][:], in_=w1_rows[:, :, a * (H // 2) : (a + 1) * (H // 2)])
         for q in range(4):
-            nc.scalar.dma_start(
+            nc.sync.dma_start(
                 out=xs_table[32 * q : 32 * q + 4, :].bitcast(I32),
                 in_=x_scales[0, 4 * q : 4 * q + 4, :].bitcast(I32),
             )
@@ -59,33 +61,34 @@ def tile_picked_unet_none_po_kernel(
         for t in range(PACK):
             nc.vector.memset(windows[t][:], 0.0)
 
-        def deal_views(raw, dealt):
-            src = raw[:].rearrange("p j (m t) -> p m t j", t=PACK)
-            dst = dealt[:].rearrange("p (t m j) -> p m t j", t=PACK, j=PACK)
-            return src, dst
+        def raw_view(raw):
+            return raw[:].rearrange("p j (m t) -> p m t j", t=PACK)
+
+        def dealt_view(dealt):
+            return dealt[:].rearrange("p (t m j) -> p m t j", t=PACK, j=PACK)
 
         def quantize(codes, scales, values):
             nc.vector.quantize_mx(out=codes.bitcast(FP8X4), scales=scales, in_=values)
 
-        xs = sb("xs", [P, S], U8)
-        nc.vector.tensor_copy(out=xs[:], in_=xs_table[:].indirect(offs_t[:]))
-
         w1_dealt = sb("w1_dealt", [P, PACK * H], BF16)
         w1_codes = sb("w1_codes", [P, H], U32)
         w1_scales = sb("w1_scales", [P, H], U8)
-        src, dst = deal_views(w1_raw, w1_dealt)
-        nc.vector.tensor_copy(out=dst[:, :W1_SPLIT], in_=src[:, :W1_SPLIT])
-        nc.scalar.activation(out=dst[:, W1_SPLIT:], in_=src[:, W1_SPLIT:], func=COPY)
+        nc.scalar.activation(out=dealt_view(w1_dealt)[:, : P // 2], in_=raw_view(w1_raw[0]), func=COPY)
+        nc.vector.tensor_copy(out=dealt_view(w1_dealt)[:, P // 2 + W1_SCALAR :], in_=raw_view(w1_raw[1])[:, W1_SCALAR:])
+        nc.scalar.copy(out=dealt_view(w1_dealt)[:, P // 2 : P // 2 + W1_SCALAR], in_=raw_view(w1_raw[1])[:, :W1_SCALAR])
+        xs = sb("xs", [P, S], U8)
+        nc.vector.tensor_copy(out=xs[:], in_=xs_table[:].indirect(offs_t[:]))
         quantize(w1_codes[:], w1_scales[:], w1_dealt[:])
 
         skip_rows = skip.rearrange("(p t) c -> p t c", t=PACK)
-        skip_a = sb("skip_a", [P, 2, U], F32, tag="xs_table")
-        nc.sync.dma_start(out=skip_a[:], in_=skip_rows[:, 0:2, :])
-        w2_raw = sb("w2_raw", [P, PACK, H], F32, tag="w1_raw")
+        skip_early = [sb("skip%d" % t, [P, U], F32, tag="w1_raw%d" % t) for t in range(2)]
+        for t in range(2):
+            nc.sync.dma_start(out=skip_early[t][:], in_=skip_rows[:, t, :])
+        w2_raw = sb("w2_raw", [P, PACK, H], F32, tag="xs_table")
         nc.sync.dma_start(out=w2_raw[:], in_=w2.rearrange("(p j) c -> p j c", j=PACK))
-        skip_b = sb("skip_b", [P, 2, U], F32, tag="w1_dealt")
-        nc.sync.dma_start(out=skip_b[:], in_=skip_rows[:, 2:4, :])
-        skip_t = [skip_a, skip_b]
+        skip_late = sb("skip_late", [P, 2, U], F32, tag="w1_dealt")
+        nc.sync.dma_start(out=skip_late[:], in_=skip_rows[:, 2:4, :])
+        skip_t = [skip_early[0][:], skip_early[1][:], skip_late[:, 0, :], skip_late[:, 1, :]]
 
         xw = [sb("xw%d" % s, [P, HALF], U32) for s in range(2)]
         cols = HALF // 16
@@ -128,12 +131,11 @@ def tile_picked_unet_none_po_kernel(
         z_planes = sb("z_planes", [P, PACK, U], BF16)
 
         def add_skip(t, lo, hi):
-            nc.vector.tensor_tensor(out=z_planes[:, t, lo:hi], in0=windows[t][:, lo:hi], in1=skip_t[t // 2][:, t % 2, lo:hi], op=ADD)
+            nc.vector.tensor_tensor(out=z_planes[:, t, lo:hi], in0=windows[t][:, lo:hi], in1=skip_t[t][:, lo:hi], op=ADD)
 
         w2_dealt = sb("w2_dealt", [P, PACK * H], BF16)
         w2_codes = sb("w2_codes", [P, H], U32)
         w2_scales = sb("w2_scales", [P, H], U8)
-        src2, dst2 = deal_views(w2_raw, w2_dealt)
 
         h_out("s", 0, 0)
         h_out("v", 0, 1)
@@ -142,15 +144,15 @@ def tile_picked_unet_none_po_kernel(
         h_out("s", 1, 0)
         h_out("s", 1, 1)
         scatter("s", 1, HALF, S)
-        scatter("v", 2, 0, HALF)
+        scatter("v", 2, 0, T2_SPLIT)
+        scatter("s", 2, T2_SPLIT, S)
         scatter("s", 3, 0, HALF)
-        scatter("s", 2, HALF, S)
         scatter("s", 3, HALF, S)
         add_skip(0, 0, U)
+        nc.vector.tensor_copy(out=dealt_view(w2_dealt), in_=raw_view(w2_raw))
         add_skip(1, 0, U)
-        nc.vector.tensor_copy(out=dst2[:, :W2_SPLIT], in_=src2[:, :W2_SPLIT])
+        quantize(w2_codes[:], w2_scales[:], w2_dealt[:])
         add_skip(2, 0, U)
-        nc.scalar.copy(out=dst2[:, W2_SPLIT:], in_=src2[:, W2_SPLIT:])
 
         n_chunks = U // CHUNK
         z_words = [sb("z_words%d" % c, [P, CHUNK * PACK], BF16) for c in range(n_chunks)]
@@ -164,10 +166,13 @@ def tile_picked_unet_none_po_kernel(
         out_rows = out_0.rearrange("(p t) c -> p t c", t=PACK)
         out_words = out_1[0].rearrange("p n t -> p (n t)").bitcast(I32)
 
-        def weave_z(c):
+        def weave_z(engine, c):
             src = z_planes[:, :, c * CHUNK : (c + 1) * CHUNK].rearrange("p t (c i) -> p c t i", i=4)
             dst = z_words[c][:].rearrange("p (c i t) -> p c t i", i=4, t=PACK)
-            nc.vector.tensor_copy(out=dst, in_=src)
+            if engine == "v":
+                nc.vector.tensor_copy(out=dst, in_=src)
+            else:
+                nc.scalar.copy(out=dst, in_=src)
 
         def product(c):
             for g in range(CHUNK // GROUP):
@@ -198,33 +203,52 @@ def tile_picked_unet_none_po_kernel(
         def weave_y_psum(c):
             for g in range(CHUNK // GROUP):
                 dst = y_words[c][:, g * GROUP * PACK : (g + 1) * GROUP * PACK].rearrange("p (c t) -> p c t", t=PACK)
-                nc.scalar.copy(out=dst, in_=y_bank[c, g][:].rearrange("p t c -> p c t"))
+                src = y_bank[c, g][:].rearrange("p t c -> p c t")
+                if g == 0:
+                    nc.scalar.copy(out=dst, in_=src)
+                else:
+                    nc.vector.tensor_copy(out=dst, in_=src)
 
         def quantize_y(c):
             cs = slice(c * CHUNK, (c + 1) * CHUNK)
             quantize(y_codes[:, cs], y_scales[:, cs], y_words[c][:])
 
+        def quantize_z(c):
+            quantize(z_codes[c][:], z_scales[c][:], z_words[c][:])
+
+        def store_words(lo, hi):
+            nc.sync.dma_start(out=out_words[:, lo:hi], in_=y_codes[:, lo:hi].bitcast(I32))
+
         add_skip(3, 0, CHUNK)
         add_skip(3, CHUNK, 2 * CHUNK)
-        weave_z(0)
-        quantize(w2_codes[:], w2_scales[:], w2_dealt[:])
-        for c in range(n_chunks):
-            if c + 2 < n_chunks:
-                add_skip(3, (c + 2) * CHUNK, (c + 3) * CHUNK)
-            quantize(z_codes[c][:], z_scales[c][:], z_words[c][:])
-            if c + 1 < n_chunks:
-                weave_z(c + 1)
-            product(c)
-            y_out(c)
-        weave_y_psum(n_chunks - 1)
+        weave_z("v", 0)
+        weave_z("s", 1)
+        add_skip(3, 2 * CHUNK, 3 * CHUNK)
+        quantize_z(0)
+        product(0)
+        y_out(0)
+        add_skip(3, 3 * CHUNK, 4 * CHUNK)
+        weave_z("v", 2)
+        quantize_z(1)
+        product(1)
+        y_out(1)
+        weave_z("v", 3)
+        quantize_z(2)
+        product(2)
+        y_out(2)
         weave_y_sbuf(0)
-        for c in range(n_chunks):
-            if c + 1 < n_chunks - 1:
-                weave_y_sbuf(c + 1)
-            quantize_y(c)
-            if c % 2 == 1:
-                cs = slice((c - 1) * CHUNK, (c + 1) * CHUNK)
-                nc.sync.dma_start(out=out_words[:, cs], in_=y_codes[:, cs].bitcast(I32))
+        quantize_z(3)
+        product(3)
+        y_out(3)
+        quantize_y(0)
+        weave_y_sbuf(1)
+        weave_y_sbuf(2)
+        quantize_y(1)
+        store_words(0, U // 2)
+        weave_y_psum(3)
+        quantize_y(2)
+        quantize_y(3)
+        store_words(U // 2, U)
         for q in range(4):
             queue = nc.sync if q < 2 else nc.scalar
             queue.dma_start(

@@ -13,6 +13,7 @@ U16 = mybir.dt.uint16
 U8 = mybir.dt.uint8
 FP8X4 = mybir.dt.float8_e4m3fn_x4
 ADD = mybir.AluOpType.add
+MULT = mybir.AluOpType.mult
 COPY = mybir.ActivationFunctionType.Copy
 
 P = 128
@@ -20,7 +21,6 @@ PACK = 4
 HALF = S // 2
 CHUNK = 256
 GROUP = 128
-T2_SPLIT = 128
 W1_SCALAR = 24
 
 
@@ -59,7 +59,8 @@ def tile_picked_unet_none_po_kernel(
         nc.sync.dma_start(out=cell_t[:], in_=cell)
 
         for t in range(PACK):
-            nc.vector.memset(windows[t][:], 0.0)
+            engine = nc.vector if t < 2 else nc.gpsimd
+            engine.memset(windows[t][:], 0.0)
 
         def raw_view(raw):
             return raw[:].rearrange("p j (m t) -> p m t j", t=PACK)
@@ -81,48 +82,48 @@ def tile_picked_unet_none_po_kernel(
         quantize(w1_codes[:], w1_scales[:], w1_dealt[:])
 
         skip_rows = skip.rearrange("(p t) c -> p t c", t=PACK)
-        skip_early = [sb("skip%d" % t, [P, U], F32, tag="w1_raw%d" % t) for t in range(2)]
-        for t in range(2):
-            nc.sync.dma_start(out=skip_early[t][:], in_=skip_rows[:, t, :])
-        w2_raw = sb("w2_raw", [P, PACK, H], F32, tag="xs_table")
-        nc.sync.dma_start(out=w2_raw[:], in_=w2.rearrange("(p j) c -> p j c", j=PACK))
-        skip_late = sb("skip_late", [P, 2, U], F32, tag="w1_dealt")
-        nc.sync.dma_start(out=skip_late[:], in_=skip_rows[:, 2:4, :])
-        skip_t = [skip_early[0][:], skip_early[1][:], skip_late[:, 0, :], skip_late[:, 1, :]]
+        w2_rows = w2.rearrange("(p j) c -> p j c", j=PACK)
+        w2_raw = [sb("w2_raw%d" % a, [P, PACK, H // 2], F32, tag="w1_raw%d" % a) for a in range(2)]
+        for a in range(2):
+            nc.sync.dma_start(out=w2_raw[a][:], in_=w2_rows[:, :, a * (H // 2) : (a + 1) * (H // 2)])
+        skip_pairs = [sb("skip_a", [P, 2, U], F32, tag="xs_table"), sb("skip_b", [P, 2, U], F32, tag="w1_dealt")]
+        for a in range(2):
+            nc.sync.dma_start(out=skip_pairs[a][:], in_=skip_rows[:, 2 * a : 2 * a + 2, :])
+        skip_t = [skip_pairs[t // 2][:, t % 2, :] for t in range(PACK)]
 
-        xw = [sb("xw%d" % s, [P, HALF], U32) for s in range(2)]
+        xw = sb("xw", [P, S], U32)
         cols = HALF // 16
         for s in range(2):
-            nc.vector.tensor_copy(out=xw[s][:], in_=x_table[:].indirect(offs_t[:, s * cols : (s + 1) * cols]))
+            nc.vector.tensor_copy(
+                out=xw[:, s * HALF : (s + 1) * HALF],
+                in_=x_table[:].indirect(offs_t[:, s * cols : (s + 1) * cols]),
+            )
 
+        h = [sb("h%d" % t, [P, S], F32) for t in range(PACK)]
+        pieces = [(1, 0, HALF), (0, 0, HALF), (0, HALF, S), (1, HALF, S), (2, 0, S), (3, 0, S)]
         h_bank = {}
-        for pair in range(2):
-            for s in range(2):
-                bank = psum.tile([P, 2, HALF], F32, name="h_bank%d%d" % (pair, s), tag="bank%d" % (2 * pair + s))
-                h_bank[pair, s] = bank
-                for i in range(2):
-                    t = 2 * pair + i
-                    nc.tensor.matmul_mx(
-                        out=bank[:, i, :],
-                        lhsT=w1_codes[:, t * P : (t + 1) * P].bitcast(FP8X4),
-                        lhsT_scale=w1_scales[:, t * P : (t + 1) * P],
-                        rhs=xw[s][:].bitcast(FP8X4),
-                        rhs_scale=xs[:, s * HALF : (s + 1) * HALF],
-                        start=True,
-                        stop=True,
-                    )
-        h = [sb("h%d" % pair, [P, 2, S], F32) for pair in range(2)]
+        for n, (t, lo, hi) in enumerate(pieces):
+            bank = psum.tile([P, hi - lo], F32, name="h_bank%d" % n, tag="bank%d" % n)
+            h_bank[t, lo] = bank
+            nc.tensor.matmul_mx(
+                out=bank[:],
+                lhsT=w1_codes[:, t * P : (t + 1) * P].bitcast(FP8X4),
+                lhsT_scale=w1_scales[:, t * P : (t + 1) * P],
+                rhs=xw[:, lo:hi].bitcast(FP8X4),
+                rhs_scale=xs[:, lo:hi],
+                start=True,
+                stop=True,
+            )
 
-        def h_out(engine, pair, s):
-            dst = h[pair][:, :, s * HALF : (s + 1) * HALF]
+        def h_out(engine, t, lo, hi):
             if engine == "v":
-                nc.vector.tensor_copy(out=dst, in_=h_bank[pair, s][:])
+                nc.vector.tensor_copy(out=h[t][:, lo:hi], in_=h_bank[t, lo][:])
             else:
-                nc.scalar.copy(out=dst, in_=h_bank[pair, s][:])
+                nc.scalar.copy(out=h[t][:, lo:hi], in_=h_bank[t, lo][:])
 
         def scatter(engine, t, lo, hi):
             dst = windows[t][:].indirect(cell_t[:, lo // 16 : hi // 16])
-            src = h[t // 2][:, t % 2, lo:hi]
+            src = h[t][:, lo:hi]
             if engine == "v":
                 nc.vector.tensor_copy(out=dst, in_=src)
             else:
@@ -130,28 +131,39 @@ def tile_picked_unet_none_po_kernel(
 
         z_planes = sb("z_planes", [P, PACK, U], BF16)
 
-        def add_skip(t, lo, hi):
-            nc.vector.tensor_tensor(out=z_planes[:, t, lo:hi], in0=windows[t][:, lo:hi], in1=skip_t[t][:, lo:hi], op=ADD)
+        def add_skip(t, lo, hi, engine=nc.vector):
+            engine.tensor_tensor(out=z_planes[:, t, lo:hi], in0=windows[t][:, lo:hi], in1=skip_t[t][:, lo:hi], op=ADD)
 
         w2_dealt = sb("w2_dealt", [P, PACK * H], BF16)
         w2_codes = sb("w2_codes", [P, H], U32)
         w2_scales = sb("w2_scales", [P, H], U8)
 
-        h_out("s", 0, 0)
-        h_out("v", 0, 1)
+        h_out("s", 1, 0, HALF)
+        h_out("v", 0, 0, HALF)
+        h_out("s", 0, HALF, S)
+        scatter("v", 0, 0, HALF)
         scatter("s", 1, 0, HALF)
-        scatter("v", 0, 0, S)
-        h_out("s", 1, 0)
-        h_out("s", 1, 1)
+        scatter("v", 0, HALF, S)
+        h_out("s", 1, HALF, S)
+        h_out("s", 2, 0, S)
         scatter("s", 1, HALF, S)
-        scatter("v", 2, 0, T2_SPLIT)
-        scatter("s", 2, T2_SPLIT, S)
+        h_out("s", 3, 0, S)
+        for a in range(2):
+            nc.gpsimd.tensor_scalar(
+                out=dealt_view(w2_dealt)[:, a * (P // 2) : (a + 1) * (P // 2)],
+                in0=raw_view(w2_raw[a]),
+                scalar1=1.0,
+                scalar2=0.0,
+                op0=MULT,
+                op1=ADD,
+            )
+        scatter("v", 2, 0, S)
         scatter("s", 3, 0, HALF)
         scatter("s", 3, HALF, S)
-        add_skip(0, 0, U)
-        nc.vector.tensor_copy(out=dealt_view(w2_dealt), in_=raw_view(w2_raw))
-        add_skip(1, 0, U)
+        add_skip(0, 0, U, nc.gpsimd)
+        add_skip(1, 0, U // 2, nc.gpsimd)
         quantize(w2_codes[:], w2_scales[:], w2_dealt[:])
+        add_skip(1, U // 2, U)
         add_skip(2, 0, U)
 
         n_chunks = U // CHUNK
@@ -177,7 +189,7 @@ def tile_picked_unet_none_po_kernel(
         def product(c):
             for g in range(CHUNK // GROUP):
                 n = 2 * c + g
-                bank = psum.tile([P, PACK, GROUP], F32, name="y_bank%d" % n, tag="bank%d" % ((n + 4) % 8))
+                bank = psum.tile([P, PACK, GROUP], F32, name="y_bank%d" % n, tag="bank%d" % ((n + 6) % 8))
                 y_bank[c, g] = bank
                 for t in range(PACK):
                     nc.tensor.matmul_mx(
@@ -195,19 +207,14 @@ def tile_picked_unet_none_po_kernel(
                 nc.scalar.copy(out=y[c][:, :, g * GROUP : (g + 1) * GROUP], in_=y_bank[c, g][:])
             nc.sync.dma_start(out=out_rows[:, :, c * CHUNK : (c + 1) * CHUNK], in_=y[c][:])
 
-        def weave_y_sbuf(c):
-            src = y[c][:].rearrange("p t (c i) -> p c t i", i=4)
-            dst = y_words[c][:].rearrange("p (c i t) -> p c t i", i=4, t=PACK)
+        def weave_y_sbuf(c, lo, hi):
+            src = y[c][:, :, lo:hi].rearrange("p t (c i) -> p c t i", i=4)
+            dst = y_words[c][:, lo * PACK : hi * PACK].rearrange("p (c i t) -> p c t i", i=4, t=PACK)
             nc.vector.tensor_copy(out=dst, in_=src)
 
-        def weave_y_psum(c):
-            for g in range(CHUNK // GROUP):
-                dst = y_words[c][:, g * GROUP * PACK : (g + 1) * GROUP * PACK].rearrange("p (c t) -> p c t", t=PACK)
-                src = y_bank[c, g][:].rearrange("p t c -> p c t")
-                if g == 0:
-                    nc.scalar.copy(out=dst, in_=src)
-                else:
-                    nc.vector.tensor_copy(out=dst, in_=src)
+        def weave_y_psum(c, g):
+            dst = y_words[c][:, g * GROUP * PACK : (g + 1) * GROUP * PACK].rearrange("p (c t) -> p c t", t=PACK)
+            nc.scalar.copy(out=dst, in_=y_bank[c, g][:].rearrange("p t c -> p c t"))
 
         def quantize_y(c):
             cs = slice(c * CHUNK, (c + 1) * CHUNK)
@@ -219,36 +226,27 @@ def tile_picked_unet_none_po_kernel(
         def store_words(lo, hi):
             nc.sync.dma_start(out=out_words[:, lo:hi], in_=y_codes[:, lo:hi].bitcast(I32))
 
-        add_skip(3, 0, CHUNK)
-        add_skip(3, CHUNK, 2 * CHUNK)
-        weave_z("v", 0)
+        for c in (1, 0, 3):
+            add_skip(3, c * CHUNK, (c + 1) * CHUNK)
         weave_z("s", 1)
+        weave_z("s", 3)
+        weave_z("v", 0)
         add_skip(3, 2 * CHUNK, 3 * CHUNK)
         quantize_z(0)
-        product(0)
-        y_out(0)
-        add_skip(3, 3 * CHUNK, 4 * CHUNK)
         weave_z("v", 2)
-        quantize_z(1)
-        product(1)
-        y_out(1)
-        weave_z("v", 3)
-        quantize_z(2)
-        product(2)
-        y_out(2)
-        weave_y_sbuf(0)
-        quantize_z(3)
-        product(3)
-        y_out(3)
-        quantize_y(0)
-        weave_y_sbuf(1)
-        weave_y_sbuf(2)
-        quantize_y(1)
-        store_words(0, U // 2)
-        weave_y_psum(3)
-        quantize_y(2)
-        quantize_y(3)
-        store_words(U // 2, U)
+        for c in range(1, n_chunks):
+            quantize_z(c)
+        for c in range(n_chunks):
+            product(c)
+            y_out(c)
+        weave_y_psum(n_chunks - 1, 1)
+        for c in range(n_chunks - 1):
+            weave_y_sbuf(c, 0, CHUNK)
+            quantize_y(c)
+        store_words(0, U - CHUNK)
+        weave_y_sbuf(n_chunks - 1, 0, GROUP)
+        quantize_y(n_chunks - 1)
+        store_words(U - CHUNK, U)
         for q in range(4):
             queue = nc.sync if q < 2 else nc.scalar
             queue.dma_start(

@@ -13,7 +13,6 @@ U16 = mybir.dt.uint16
 U8 = mybir.dt.uint8
 FP8X4 = mybir.dt.float8_e4m3fn_x4
 ADD = mybir.AluOpType.add
-MULT = mybir.AluOpType.mult
 COPY = mybir.ActivationFunctionType.Copy
 
 P = 128
@@ -21,7 +20,7 @@ PACK = 4
 HALF = S // 2
 CHUNK = 256
 GROUP = 128
-W1_SCALAR = 24
+W1_SCALAR = 48
 
 
 def tile_picked_unet_none_po_kernel(
@@ -39,14 +38,13 @@ def tile_picked_unet_none_po_kernel(
         cell_t = keep.tile([P, S // 16], U16, name="cell_t")
         x_table = sb("x_table", [P, T], U32)
         xs_table = sb("xs_table", [P, T], U8)
-        w1_raw = [sb("w1_raw%d" % a, [P, PACK, H // 2], F32) for a in range(2)]
+        w1_raw = sb("w1_raw", [P, PACK, H], F32)
         windows = [sb("window%d" % t, [P, U], F32) for t in range(PACK)]
 
         nc.vector.memset(xs_table[:].bitcast(I32), 0)
         nc.sync.dma_start(out=offs_t[:], in_=offs)
-        w1_rows = w1.rearrange("(p j) c -> p j c", j=PACK)
-        for a in range(2):
-            nc.sync.dma_start(out=w1_raw[a][:], in_=w1_rows[:, :, a * (H // 2) : (a + 1) * (H // 2)])
+        nc.sync.dma_start(out=cell_t[:], in_=cell)
+        nc.sync.dma_start(out=w1_raw[:], in_=w1.rearrange("(p j) c -> p j c", j=PACK))
         for q in range(4):
             nc.sync.dma_start(
                 out=xs_table[32 * q : 32 * q + 4, :].bitcast(I32),
@@ -56,17 +54,15 @@ def tile_picked_unet_none_po_kernel(
             out=x_table[:].bitcast(I32),
             in_=x_words[0].rearrange("p n t -> p (n t)").bitcast(I32),
         )
-        nc.sync.dma_start(out=cell_t[:], in_=cell)
 
         for t in range(PACK):
-            engine = nc.vector if t < 2 else nc.gpsimd
-            engine.memset(windows[t][:], 0.0)
+            nc.vector.memset(windows[t][:].bitcast(I32), 0)
 
         def raw_view(raw):
-            return raw[:].rearrange("p j (m t) -> p m t j", t=PACK)
+            return raw[:].rearrange("p j (m t) -> p m j t", t=PACK)
 
         def dealt_view(dealt):
-            return dealt[:].rearrange("p (t m j) -> p m t j", t=PACK, j=PACK)
+            return dealt[:].rearrange("p (t m j) -> p m j t", t=PACK, j=PACK)
 
         def quantize(codes, scales, values):
             nc.vector.quantize_mx(out=codes.bitcast(FP8X4), scales=scales, in_=values)
@@ -74,22 +70,11 @@ def tile_picked_unet_none_po_kernel(
         w1_dealt = sb("w1_dealt", [P, PACK * H], BF16)
         w1_codes = sb("w1_codes", [P, H], U32)
         w1_scales = sb("w1_scales", [P, H], U8)
-        nc.scalar.activation(out=dealt_view(w1_dealt)[:, : P // 2], in_=raw_view(w1_raw[0]), func=COPY)
-        nc.vector.tensor_copy(out=dealt_view(w1_dealt)[:, P // 2 + W1_SCALAR :], in_=raw_view(w1_raw[1])[:, W1_SCALAR:])
-        nc.scalar.copy(out=dealt_view(w1_dealt)[:, P // 2 : P // 2 + W1_SCALAR], in_=raw_view(w1_raw[1])[:, :W1_SCALAR])
+        nc.vector.tensor_copy(out=dealt_view(w1_dealt)[:, W1_SCALAR:], in_=raw_view(w1_raw)[:, W1_SCALAR:])
+        nc.scalar.activation(out=dealt_view(w1_dealt)[:, :W1_SCALAR], in_=raw_view(w1_raw)[:, :W1_SCALAR], func=COPY)
         xs = sb("xs", [P, S], U8)
         nc.vector.tensor_copy(out=xs[:], in_=xs_table[:].indirect(offs_t[:]))
-        quantize(w1_codes[:], w1_scales[:], w1_dealt[:])
-
-        skip_rows = skip.rearrange("(p t) c -> p t c", t=PACK)
-        w2_rows = w2.rearrange("(p j) c -> p j c", j=PACK)
-        w2_raw = [sb("w2_raw%d" % a, [P, PACK, H // 2], F32, tag="w1_raw%d" % a) for a in range(2)]
-        for a in range(2):
-            nc.sync.dma_start(out=w2_raw[a][:], in_=w2_rows[:, :, a * (H // 2) : (a + 1) * (H // 2)])
-        skip_pairs = [sb("skip_a", [P, 2, U], F32, tag="xs_table"), sb("skip_b", [P, 2, U], F32, tag="w1_dealt")]
-        for a in range(2):
-            nc.sync.dma_start(out=skip_pairs[a][:], in_=skip_rows[:, 2 * a : 2 * a + 2, :])
-        skip_t = [skip_pairs[t // 2][:, t % 2, :] for t in range(PACK)]
+        quantize(w1_codes[:, : H // 2], w1_scales[:, : H // 2], w1_dealt[:, : PACK * H // 2])
 
         xw = sb("xw", [P, S], U32)
         cols = HALF // 16
@@ -99,8 +84,19 @@ def tile_picked_unet_none_po_kernel(
                 in_=x_table[:].indirect(offs_t[:, s * cols : (s + 1) * cols]),
             )
 
-        h = [sb("h%d" % t, [P, S], F32) for t in range(PACK)]
-        pieces = [(1, 0, HALF), (0, 0, HALF), (0, HALF, S), (1, HALF, S), (2, 0, S), (3, 0, S)]
+        quantize(w1_codes[:, H // 2 :], w1_scales[:, H // 2 :], w1_dealt[:, PACK * H // 2 :])
+
+        skip_rows = skip.rearrange("(p t) c -> p t c", t=PACK)
+        skip_a = sb("skip_a", [P, 2, U], F32, tag="w1_raw")
+        nc.sync.dma_start(out=skip_a[:], in_=skip_rows[:, 0:2, :])
+        w2_raw = sb("w2_raw", [P, PACK, H], F32, tag="xs_table")
+        nc.sync.dma_start(out=w2_raw[:], in_=w2.rearrange("(p j) c -> p j c", j=PACK))
+        skip_b = sb("skip_b", [P, 2, U], F32, tag="w1_dealt")
+        nc.sync.dma_start(out=skip_b[:], in_=skip_rows[:, 2:4, :])
+        skip_t = [skip_a[:, 0, :], skip_a[:, 1, :], skip_b[:, 0, :], skip_b[:, 1, :]]
+
+        h = {}
+        pieces = [(1, 0, HALF), (0, 0, HALF), (0, HALF, S), (1, HALF, S), (3, 0, HALF), (2, 0, S), (3, HALF, S)]
         h_bank = {}
         for n, (t, lo, hi) in enumerate(pieces):
             bank = psum.tile([P, hi - lo], F32, name="h_bank%d" % n, tag="bank%d" % n)
@@ -115,15 +111,18 @@ def tile_picked_unet_none_po_kernel(
                 stop=True,
             )
 
-        def h_out(engine, t, lo, hi):
+        def h_out(engine, t, lo, hi, tag=None):
+            piece = sb("h%d_%d" % (t, lo), [P, hi - lo], F32, tag=tag)
+            for start in range(lo, hi, HALF):
+                h[t, start] = piece[:, start - lo : start - lo + HALF]
             if engine == "v":
-                nc.vector.tensor_copy(out=h[t][:, lo:hi], in_=h_bank[t, lo][:])
+                nc.vector.tensor_copy(out=piece[:], in_=h_bank[t, lo][:])
             else:
-                nc.scalar.copy(out=h[t][:, lo:hi], in_=h_bank[t, lo][:])
+                nc.scalar.copy(out=piece[:], in_=h_bank[t, lo][:])
 
         def scatter(engine, t, lo, hi):
             dst = windows[t][:].indirect(cell_t[:, lo // 16 : hi // 16])
-            src = h[t][:, lo:hi]
+            src = h[t, lo]
             if engine == "v":
                 nc.vector.tensor_copy(out=dst, in_=src)
             else:
@@ -131,8 +130,8 @@ def tile_picked_unet_none_po_kernel(
 
         z_planes = sb("z_planes", [P, PACK, U], BF16)
 
-        def add_skip(t, lo, hi, engine=nc.vector):
-            engine.tensor_tensor(out=z_planes[:, t, lo:hi], in0=windows[t][:, lo:hi], in1=skip_t[t][:, lo:hi], op=ADD)
+        def add_skip(t, lo, hi):
+            nc.vector.tensor_tensor(out=z_planes[:, t, lo:hi], in0=windows[t][:, lo:hi], in1=skip_t[t][:, lo:hi], op=ADD)
 
         w2_dealt = sb("w2_dealt", [P, PACK * H], BF16)
         w2_codes = sb("w2_codes", [P, H], U32)
@@ -145,26 +144,19 @@ def tile_picked_unet_none_po_kernel(
         scatter("s", 1, 0, HALF)
         scatter("v", 0, HALF, S)
         h_out("s", 1, HALF, S)
-        h_out("s", 2, 0, S)
         scatter("s", 1, HALF, S)
-        h_out("s", 3, 0, S)
-        for a in range(2):
-            nc.gpsimd.tensor_scalar(
-                out=dealt_view(w2_dealt)[:, a * (P // 2) : (a + 1) * (P // 2)],
-                in0=raw_view(w2_raw[a]),
-                scalar1=1.0,
-                scalar2=0.0,
-                op0=MULT,
-                op1=ADD,
-            )
-        scatter("v", 2, 0, S)
-        scatter("s", 3, 0, HALF)
+        h_out("s", 3, 0, HALF)
+        h_out("s", 2, 0, S)
+        scatter("v", 3, 0, HALF)
+        scatter("s", 2, 0, HALF)
+        scatter("s", 2, HALF, S)
+        h_out("s", 3, HALF, S, tag="h2_0")
         scatter("s", 3, HALF, S)
-        add_skip(0, 0, U, nc.gpsimd)
-        add_skip(1, 0, U // 2, nc.gpsimd)
-        quantize(w2_codes[:], w2_scales[:], w2_dealt[:])
-        add_skip(1, U // 2, U)
+        add_skip(0, 0, U)
+        add_skip(1, 0, U)
+        nc.vector.tensor_copy(out=dealt_view(w2_dealt), in_=raw_view(w2_raw))
         add_skip(2, 0, U)
+        quantize(w2_codes[:], w2_scales[:], w2_dealt[:])
 
         n_chunks = U // CHUNK
         z_words = [sb("z_words%d" % c, [P, CHUNK * PACK], BF16) for c in range(n_chunks)]
@@ -178,34 +170,39 @@ def tile_picked_unet_none_po_kernel(
         out_rows = out_0.rearrange("(p t) c -> p t c", t=PACK)
         out_words = out_1[0].rearrange("p n t -> p (n t)").bitcast(I32)
 
-        def weave_z(engine, c):
-            src = z_planes[:, :, c * CHUNK : (c + 1) * CHUNK].rearrange("p t (c i) -> p c t i", i=4)
-            dst = z_words[c][:].rearrange("p (c i t) -> p c t i", i=4, t=PACK)
+        def weave_z(engine, lo, hi):
+            c, at = divmod(lo, CHUNK)
+            src = z_planes[:, :, lo:hi].rearrange("p t (c i) -> p c t i", i=4)
+            dst = z_words[c][:, at * PACK : (at + hi - lo) * PACK].rearrange("p (c i t) -> p c t i", i=4, t=PACK)
             if engine == "v":
                 nc.vector.tensor_copy(out=dst, in_=src)
             else:
                 nc.scalar.copy(out=dst, in_=src)
 
-        def product(c):
-            for g in range(CHUNK // GROUP):
+        def quantize_z(lo, hi):
+            c, at = divmod(lo, CHUNK)
+            end = at + hi - lo
+            quantize(z_codes[c][:, at:end], z_scales[c][:, at:end], z_words[c][:, at * PACK : end * PACK])
+
+        def product_and_store(lo, hi):
+            c, at = divmod(lo, CHUNK)
+            for start in range(at, at + hi - lo, GROUP):
+                g = start // GROUP
                 n = 2 * c + g
-                bank = psum.tile([P, PACK, GROUP], F32, name="y_bank%d" % n, tag="bank%d" % ((n + 6) % 8))
+                bank = psum.tile([P, PACK, GROUP], F32, name="y_bank%d" % n, tag="bank%d" % ((n + 7) % 8))
                 y_bank[c, g] = bank
                 for t in range(PACK):
                     nc.tensor.matmul_mx(
                         out=bank[:, t, :],
                         lhsT=w2_codes[:, t * P : (t + 1) * P].bitcast(FP8X4),
                         lhsT_scale=w2_scales[:, t * P : (t + 1) * P],
-                        rhs=z_codes[c][:, g * GROUP : (g + 1) * GROUP].bitcast(FP8X4),
-                        rhs_scale=z_scales[c][:, g * GROUP : (g + 1) * GROUP],
+                        rhs=z_codes[c][:, start : start + GROUP].bitcast(FP8X4),
+                        rhs_scale=z_scales[c][:, start : start + GROUP],
                         start=True,
                         stop=True,
                     )
-
-        def y_out(c):
-            for g in range(CHUNK // GROUP):
-                nc.scalar.copy(out=y[c][:, :, g * GROUP : (g + 1) * GROUP], in_=y_bank[c, g][:])
-            nc.sync.dma_start(out=out_rows[:, :, c * CHUNK : (c + 1) * CHUNK], in_=y[c][:])
+                nc.scalar.copy(out=y[c][:, :, start : start + GROUP], in_=bank[:])
+            nc.sync.dma_start(out=out_rows[:, :, lo:hi], in_=y[c][:, :, at : at + hi - lo])
 
         def weave_y_sbuf(c, lo, hi):
             src = y[c][:, :, lo:hi].rearrange("p t (c i) -> p c t i", i=4)
@@ -220,31 +217,36 @@ def tile_picked_unet_none_po_kernel(
             cs = slice(c * CHUNK, (c + 1) * CHUNK)
             quantize(y_codes[:, cs], y_scales[:, cs], y_words[c][:])
 
-        def quantize_z(c):
-            quantize(z_codes[c][:], z_scales[c][:], z_words[c][:])
-
         def store_words(lo, hi):
             nc.sync.dma_start(out=out_words[:, lo:hi], in_=y_codes[:, lo:hi].bitcast(I32))
 
-        for c in (1, 0, 3):
-            add_skip(3, c * CHUNK, (c + 1) * CHUNK)
-        weave_z("s", 1)
-        weave_z("s", 3)
-        weave_z("v", 0)
-        add_skip(3, 2 * CHUNK, 3 * CHUNK)
-        quantize_z(0)
-        weave_z("v", 2)
-        for c in range(1, n_chunks):
-            quantize_z(c)
-        for c in range(n_chunks):
-            product(c)
-            y_out(c)
-        weave_y_psum(n_chunks - 1, 1)
-        for c in range(n_chunks - 1):
-            weave_y_sbuf(c, 0, CHUNK)
-            quantize_y(c)
+        add_skip(3, 0, 128)
+        add_skip(3, 128, 512)
+        weave_z("v", 0, 128)
+        weave_z("s", 256, 512)
+        add_skip(3, 512, 1024)
+        quantize_z(0, 128)
+        product_and_store(0, 128)
+        weave_z("v", 128, 256)
+        weave_z("v", 512, 768)
+        quantize_z(128, 256)
+        product_and_store(128, 256)
+        quantize_z(256, 512)
+        product_and_store(256, 512)
+        quantize_z(512, 768)
+        product_and_store(512, 768)
+        weave_z("v", 768, 1024)
+        weave_y_sbuf(0, 0, CHUNK)
+        quantize_z(768, 1024)
+        product_and_store(768, 1024)
+        for g in range(2):
+            weave_y_psum(n_chunks - 1, g)
+        quantize_y(0)
+        weave_y_sbuf(1, 0, CHUNK)
+        quantize_y(1)
+        weave_y_sbuf(2, 0, CHUNK)
+        quantize_y(2)
         store_words(0, U - CHUNK)
-        weave_y_sbuf(n_chunks - 1, 0, GROUP)
         quantize_y(n_chunks - 1)
         store_words(U - CHUNK, U)
         for q in range(4):

from contextlib import ExitStack

import concourse.mybir as mybir

K, T, S, H, U = 512, 2048, 512, 512, 1024
FLOPS = 2 * K * H * S + 2 * H * H * U

F32 = mybir.dt.float32
BF16 = mybir.dt.bfloat16
I32 = mybir.dt.int32
U32 = mybir.dt.uint32
U16 = mybir.dt.uint16
U8 = mybir.dt.uint8
FP8X4 = mybir.dt.float8_e4m3fn_x4
ADD = mybir.AluOpType.add
COPY = mybir.ActivationFunctionType.Copy

P = 128
PACK = 4
HALF = S // 2
CHUNK = 256
GROUP = 128
W1_SCALAR = 48


def tile_picked_unet_none_po_kernel(
    tc, x_words, x_scales, w1, w2, skip, offs, cell, out_0, out_1, out_2
):
    nc = tc.nc
    with ExitStack() as ctx:
        keep = ctx.enter_context(tc.tile_pool(name="keep", bufs=1))
        psum = ctx.enter_context(tc.psum_pool(name="psum", bufs=1))

        def sb(name, shape, dtype, tag=None):
            return keep.tile(shape, dtype, name=name, tag=tag or name, align_bytes=64)

        offs_t = keep.tile([P, S // 16], U16, name="offs_t")
        cell_t = keep.tile([P, S // 16], U16, name="cell_t")
        x_table = sb("x_table", [P, T], U32)
        xs_table = sb("xs_table", [P, T], U8)
        w1_raw = sb("w1_raw", [P, PACK, H], F32)
        windows = [sb("window%d" % t, [P, U], F32) for t in range(PACK)]

        nc.vector.memset(xs_table[:].bitcast(I32), 0)
        nc.sync.dma_start(out=offs_t[:], in_=offs)
        nc.sync.dma_start(out=cell_t[:], in_=cell)
        nc.sync.dma_start(out=w1_raw[:], in_=w1.rearrange("(p j) c -> p j c", j=PACK))
        for q in range(4):
            nc.sync.dma_start(
                out=xs_table[32 * q : 32 * q + 4, :].bitcast(I32),
                in_=x_scales[0, 4 * q : 4 * q + 4, :].bitcast(I32),
            )
        nc.sync.dma_start(
            out=x_table[:].bitcast(I32),
            in_=x_words[0].rearrange("p n t -> p (n t)").bitcast(I32),
        )

        for t in range(PACK):
            nc.vector.memset(windows[t][:].bitcast(I32), 0)

        def raw_view(raw):
            return raw[:].rearrange("p j (m t) -> p m j t", t=PACK)

        def dealt_view(dealt):
            return dealt[:].rearrange("p (t m j) -> p m j t", t=PACK, j=PACK)

        def quantize(codes, scales, values):
            nc.vector.quantize_mx(out=codes.bitcast(FP8X4), scales=scales, in_=values)

        w1_dealt = sb("w1_dealt", [P, PACK * H], BF16)
        w1_codes = sb("w1_codes", [P, H], U32)
        w1_scales = sb("w1_scales", [P, H], U8)
        nc.vector.tensor_copy(out=dealt_view(w1_dealt)[:, W1_SCALAR:], in_=raw_view(w1_raw)[:, W1_SCALAR:])
        nc.scalar.activation(out=dealt_view(w1_dealt)[:, :W1_SCALAR], in_=raw_view(w1_raw)[:, :W1_SCALAR], func=COPY)
        xs = sb("xs", [P, S], U8)
        nc.vector.tensor_copy(out=xs[:], in_=xs_table[:].indirect(offs_t[:]))
        quantize(w1_codes[:, : H // 2], w1_scales[:, : H // 2], w1_dealt[:, : PACK * H // 2])

        xw = sb("xw", [P, S], U32)
        cols = HALF // 16
        for s in range(2):
            nc.vector.tensor_copy(
                out=xw[:, s * HALF : (s + 1) * HALF],
                in_=x_table[:].indirect(offs_t[:, s * cols : (s + 1) * cols]),
            )

        quantize(w1_codes[:, H // 2 :], w1_scales[:, H // 2 :], w1_dealt[:, PACK * H // 2 :])

        skip_rows = skip.rearrange("(p t) c -> p t c", t=PACK)
        skip_a = sb("skip_a", [P, 2, U], F32, tag="w1_raw")
        nc.sync.dma_start(out=skip_a[:], in_=skip_rows[:, 0:2, :])
        w2_raw = sb("w2_raw", [P, PACK, H], F32, tag="xs_table")
        nc.sync.dma_start(out=w2_raw[:], in_=w2.rearrange("(p j) c -> p j c", j=PACK))
        skip_b = sb("skip_b", [P, 2, U], F32, tag="w1_dealt")
        nc.sync.dma_start(out=skip_b[:], in_=skip_rows[:, 2:4, :])
        skip_t = [skip_a[:, 0, :], skip_a[:, 1, :], skip_b[:, 0, :], skip_b[:, 1, :]]

        h = {}
        pieces = [(1, 0, HALF), (0, 0, HALF), (0, HALF, S), (1, HALF, S), (3, 0, HALF), (2, 0, S), (3, HALF, S)]
        h_bank = {}
        for n, (t, lo, hi) in enumerate(pieces):
            bank = psum.tile([P, hi - lo], F32, name="h_bank%d" % n, tag="bank%d" % n)
            h_bank[t, lo] = bank
            nc.tensor.matmul_mx(
                out=bank[:],
                lhsT=w1_codes[:, t * P : (t + 1) * P].bitcast(FP8X4),
                lhsT_scale=w1_scales[:, t * P : (t + 1) * P],
                rhs=xw[:, lo:hi].bitcast(FP8X4),
                rhs_scale=xs[:, lo:hi],
                start=True,
                stop=True,
            )

        def h_out(engine, t, lo, hi, tag=None):
            piece = sb("h%d_%d" % (t, lo), [P, hi - lo], F32, tag=tag)
            for start in range(lo, hi, HALF):
                h[t, start] = piece[:, start - lo : start - lo + HALF]
            if engine == "v":
                nc.vector.tensor_copy(out=piece[:], in_=h_bank[t, lo][:])
            else:
                nc.scalar.copy(out=piece[:], in_=h_bank[t, lo][:])

        def scatter(engine, t, lo, hi):
            dst = windows[t][:].indirect(cell_t[:, lo // 16 : hi // 16])
            src = h[t, lo]
            if engine == "v":
                nc.vector.tensor_copy(out=dst, in_=src)
            else:
                nc.scalar.activation(out=dst, in_=src, func=COPY)

        z_planes = sb("z_planes", [P, PACK, U], BF16)

        def add_skip(t, lo, hi):
            nc.vector.tensor_tensor(out=z_planes[:, t, lo:hi], in0=windows[t][:, lo:hi], in1=skip_t[t][:, lo:hi], op=ADD)

        w2_dealt = sb("w2_dealt", [P, PACK * H], BF16)
        w2_codes = sb("w2_codes", [P, H], U32)
        w2_scales = sb("w2_scales", [P, H], U8)

        h_out("s", 1, 0, HALF)
        h_out("v", 0, 0, HALF)
        h_out("s", 0, HALF, S)
        scatter("v", 0, 0, HALF)
        scatter("s", 1, 0, HALF)
        scatter("v", 0, HALF, S)
        h_out("s", 1, HALF, S)
        scatter("s", 1, HALF, S)
        h_out("s", 3, 0, HALF)
        h_out("s", 2, 0, S)
        scatter("v", 3, 0, HALF)
        scatter("s", 2, 0, HALF)
        scatter("s", 2, HALF, S)
        h_out("s", 3, HALF, S, tag="h2_0")
        scatter("s", 3, HALF, S)
        add_skip(0, 0, U)
        add_skip(1, 0, U)
        nc.vector.tensor_copy(out=dealt_view(w2_dealt), in_=raw_view(w2_raw))
        add_skip(2, 0, U)
        quantize(w2_codes[:], w2_scales[:], w2_dealt[:])

        n_chunks = U // CHUNK
        z_words = [sb("z_words%d" % c, [P, CHUNK * PACK], BF16) for c in range(n_chunks)]
        z_codes = [sb("z_codes%d" % c, [P, CHUNK], U32) for c in range(n_chunks)]
        z_scales = [sb("z_scales%d" % c, [P, CHUNK], U8) for c in range(n_chunks)]
        y = [sb("y%d" % c, [P, PACK, CHUNK], F32) for c in range(n_chunks)]
        y_words = [sb("y_words%d" % c, [P, CHUNK * PACK], BF16) for c in range(n_chunks)]
        y_codes = sb("y_codes", [P, U], U32)
        y_scales = sb("y_scales", [P, U], U8)
        y_bank = {}
        out_rows = out_0.rearrange("(p t) c -> p t c", t=PACK)
        out_words = out_1[0].rearrange("p n t -> p (n t)").bitcast(I32)

        def weave_z(engine, lo, hi):
            c, at = divmod(lo, CHUNK)
            src = z_planes[:, :, lo:hi].rearrange("p t (c i) -> p c t i", i=4)
            dst = z_words[c][:, at * PACK : (at + hi - lo) * PACK].rearrange("p (c i t) -> p c t i", i=4, t=PACK)
            if engine == "v":
                nc.vector.tensor_copy(out=dst, in_=src)
            else:
                nc.scalar.copy(out=dst, in_=src)

        def quantize_z(lo, hi):
            c, at = divmod(lo, CHUNK)
            end = at + hi - lo
            quantize(z_codes[c][:, at:end], z_scales[c][:, at:end], z_words[c][:, at * PACK : end * PACK])

        def product_and_store(lo, hi):
            c, at = divmod(lo, CHUNK)
            for start in range(at, at + hi - lo, GROUP):
                g = start // GROUP
                n = 2 * c + g
                bank = psum.tile([P, PACK, GROUP], F32, name="y_bank%d" % n, tag="bank%d" % ((n + 7) % 8))
                y_bank[c, g] = bank
                for t in range(PACK):
                    nc.tensor.matmul_mx(
                        out=bank[:, t, :],
                        lhsT=w2_codes[:, t * P : (t + 1) * P].bitcast(FP8X4),
                        lhsT_scale=w2_scales[:, t * P : (t + 1) * P],
                        rhs=z_codes[c][:, start : start + GROUP].bitcast(FP8X4),
                        rhs_scale=z_scales[c][:, start : start + GROUP],
                        start=True,
                        stop=True,
                    )
                nc.scalar.copy(out=y[c][:, :, start : start + GROUP], in_=bank[:])
            nc.sync.dma_start(out=out_rows[:, :, lo:hi], in_=y[c][:, :, at : at + hi - lo])

        def weave_y_sbuf(c, lo, hi):
            src = y[c][:, :, lo:hi].rearrange("p t (c i) -> p c t i", i=4)
            dst = y_words[c][:, lo * PACK : hi * PACK].rearrange("p (c i t) -> p c t i", i=4, t=PACK)
            nc.vector.tensor_copy(out=dst, in_=src)

        def weave_y_psum(c, g):
            dst = y_words[c][:, g * GROUP * PACK : (g + 1) * GROUP * PACK].rearrange("p (c t) -> p c t", t=PACK)
            nc.scalar.copy(out=dst, in_=y_bank[c, g][:].rearrange("p t c -> p c t"))

        def quantize_y(c):
            cs = slice(c * CHUNK, (c + 1) * CHUNK)
            quantize(y_codes[:, cs], y_scales[:, cs], y_words[c][:])

        def store_words(lo, hi):
            nc.sync.dma_start(out=out_words[:, lo:hi], in_=y_codes[:, lo:hi].bitcast(I32))

        add_skip(3, 0, 128)
        add_skip(3, 128, 512)
        weave_z("v", 0, 128)
        weave_z("s", 256, 512)
        add_skip(3, 512, 1024)
        quantize_z(0, 128)
        product_and_store(0, 128)
        weave_z("v", 128, 256)
        weave_z("v", 512, 768)
        quantize_z(128, 256)
        product_and_store(128, 256)
        quantize_z(256, 512)
        product_and_store(256, 512)
        quantize_z(512, 768)
        product_and_store(512, 768)
        weave_z("v", 768, 1024)
        weave_y_sbuf(0, 0, CHUNK)
        quantize_z(768, 1024)
        product_and_store(768, 1024)
        for g in range(2):
            weave_y_psum(n_chunks - 1, g)
        quantize_y(0)
        weave_y_sbuf(1, 0, CHUNK)
        quantize_y(1)
        weave_y_sbuf(2, 0, CHUNK)
        quantize_y(2)
        store_words(0, U - CHUNK)
        quantize_y(n_chunks - 1)
        store_words(U - CHUNK, U)
        for q in range(4):
            queue = nc.sync if q < 2 else nc.scalar
            queue.dma_start(
                out=out_2[0, 4 * q : 4 * q + 4, :].bitcast(I32),
                in_=y_scales[32 * q : 32 * q + 4, :].bitcast(I32),
            )
